import numpy as np
import ml_dtypes


def mxq(x, axis, fmt="e4m3"):
    dtype, down = {"e4m3": (ml_dtypes.float8_e4m3fn, 7), "e5m2": (ml_dtypes.float8_e5m2, 14)}[fmt]
    v = np.moveaxis(np.asarray(x, np.float32).astype(ml_dtypes.bfloat16).astype(np.float64), axis, -1)
    blocks = v.reshape(v.shape[:-1] + (-1, 32))
    amax = np.abs(blocks).max(-1, keepdims=True)
    byte = np.maximum(np.where(amax > 0, np.frexp(amax)[1] - 1 + 127, 0) - down, 1)
    scale = np.exp2(byte - 127.0)
    codes = (blocks / scale).astype(np.float32).astype(dtype).astype(np.float64)
    return np.moveaxis((codes * scale).reshape(v.shape), -1, axis)


WIDE = False


def mx_kscale(k):
    if not WIDE:
        return np.ones(k)
    levels = np.array([10, -10, 5, -5, 0])
    if k % 512:
        return np.exp2(np.random.permutation(np.resize(levels, k // 32))).repeat(32)
    a = np.empty((k // 512, 16))
    for p in range(k // 512):
        a[p, :8] = np.random.permutation(np.resize(levels, 8))
        for g in range(8):
            far = levels[np.abs(levels - a[p, g]) >= 10]
            a[p, g + 8] = far[np.random.randint(len(far))]
    return np.exp2(a.ravel()).repeat(32)


def f64(x):
    return np.asarray(x).astype(np.float64)


def striped(idx):
    return np.tile(idx.reshape(-1, 16).T, (8, 1)).astype(np.uint16)


def unstriped(offs):
    return offs[:16].T.reshape(-1).astype(np.int64)


def relu(v):
    return np.maximum(v, 0.0)


K, T, D, S, V, H, N = 1024, 2048, 3, 512, 256, 512, 128
P = 2 ** 7


def setup_inputs():
    n = np.random.standard_normal
    s = mx_kscale(K)[:, None]
    u = mx_kscale(H)
    q = np.random.permutation(S)
    return {
        "xT": (n((K, T)) * s).astype(np.float32),
        "w1": (n((K, H)) / np.sqrt(K) / s * u).astype(np.float32),
        "w2": (n((H, N)) / np.sqrt(H) / u[:, None]).astype(np.float32),
        "gate": np.tile(np.random.uniform(0.2, 1.0, (D, 1, V)) / np.sqrt(D), (1, P, 1)).astype(np.float32),
        "offs": striped(np.random.permutation(T)[:S]),
        "pos1": striped(q[:V]),
        "pos2": striped(q[V:]),
        "pos3": striped(np.random.permutation(S)[:V]),
    }


def reference(xT, w1, w2, gate, offs, pos1, pos2, pos3):
    h = relu(mxq(f64(w1), 0, "e4m3").T @ mxq(f64(xT)[:, unstriped(offs)], 0, "e4m3"))
    z = sum(f64(gate)[d, :1] * h[:, unstriped(p)] for d, p in enumerate((pos1, pos2, pos3)))
    return mxq(f64(w2), 0, "e4m3").T @ mxq(z, 0, "e4m3")

@@ -1,0 +1,171 @@
+from contextlib import ExitStack
+
+import concourse.mybir as mybir
+
+K, T, D, S, V, H, N = 1024, 2048, 3, 512, 256, 512, 128
+P = 128
+PACK = 4
+PASSES = K // (P * PACK)
+FLOPS = 2 * K * S * H + 2 * H * V * N
+
+F32 = mybir.dt.float32
+BF16 = mybir.dt.bfloat16
+U32 = mybir.dt.uint32
+U16 = mybir.dt.uint16
+U8 = mybir.dt.uint8
+FP8X4 = mybir.dt.float8_e4m3fn_x4
+ADD = mybir.AluOpType.add
+MULT = mybir.AluOpType.mult
+RELU = mybir.ActivationFunctionType.Relu
+
+
+def tile_picked_sage_relu_e_kernel(tc, xT, w1, w2, gate, offs, pos1, pos2, pos3, out):
+    nc = tc.nc
+    with ExitStack() as ctx:
+        keep = ctx.enter_context(tc.tile_pool(name="keep", bufs=1))
+        psum = ctx.enter_context(tc.psum_pool(name="psum", bufs=1))
+
+        offs_t = keep.tile([P, S // 16], U16, name="offs_t")
+        pos_t = [keep.tile([P, V // 16], U16, name=f"pos_t{d}") for d in range(D)]
+        nc.sync.dma_start(offs_t[:], offs)
+
+        planes = xT.rearrange("(s p j) t -> s j p t", p=P, j=PACK)
+        w1_rows = w1.rearrange("(s p j) c -> s p j c", p=P, j=PACK)
+        xs = [[keep.tile([P, T], F32, name=f"x{s}_{j}") for j in range(PACK)] for s in range(PASSES)]
+        w1_raw = [keep.tile([P, PACK, H], F32, name="w1_raw0")]
+        halves = [keep.tile([P, PACK, H // 2], F32, name=f"w1_raw1_{u}") for u in range(2)]
+        w2_raw = keep.tile([P, PACK, N], F32, name="w2_raw")
+        gates = keep.tile([P, D, V], F32, name="gates")
+
+        nc.sync.dma_start(xs[0][0][:], planes[0, 0])
+        for d, p in enumerate((pos1, pos2, pos3)):
+            nc.sync.dma_start(pos_t[d][:], p)
+        for i in range(1, PASSES * PACK):
+            nc.sync.dma_start(xs[i // PACK][i % PACK][:], planes[i // PACK, i % PACK])
+        nc.sync.dma_start(w1_raw[0][:], w1_rows[0])
+        for u in range(2):
+            nc.sync.dma_start(halves[u][:], w1_rows[1][:, :, u * (H // 2) : (u + 1) * (H // 2)])
+        nc.sync.dma_start(gates[:], gate.rearrange("d p v -> p d v"))
+        nc.sync.dma_start(w2_raw[:], w2.rearrange("(p j) m -> p j m", j=PACK))
+
+        xg = [keep.tile([P, S, PACK], BF16, name=f"xg{s}", align_bytes=64) for s in range(PASSES)]
+        x_codes = [keep.tile([P, S], U32, name=f"x_codes{s}", align_bytes=64) for s in range(PASSES)]
+        x_scales = [keep.tile([P, S], U8, name=f"x_scales{s}", align_bytes=64) for s in range(PASSES)]
+        w1g = [keep.tile([P, H * PACK], BF16, name=f"w1g{s}", align_bytes=64) for s in range(PASSES)]
+        w1_codes = [keep.tile([P, H], U32, name=f"w1_codes{s}", align_bytes=64) for s in range(PASSES)]
+        w1_scales = [keep.tile([P, H], U8, name=f"w1_scales{s}", align_bytes=64) for s in range(PASSES)]
+
+        def quantize(codes, scales, grouped):
+            nc.vector.quantize_mx(out=codes.bitcast(FP8X4), scales=scales, in_=grouped)
+
+        def quantize_x(s):
+            quantize(x_codes[s][:], x_scales[s][:], xg[s][:].rearrange("p n j -> p (n j)"))
+
+        for i in range(PASSES * PACK):
+            s, j = i // PACK, i % PACK
+            nc.vector.tensor_copy(xg[s][:, :, j], xs[s][j][:].indirect(offs_t[:]))
+            if i == PACK:
+                quantize_x(0)
+
+        def lay(engine, s, raw, m0, m1, t0, t1):
+            base = 0 if raw is w1_raw[0] else m0
+            dst = w1g[s][:].rearrange("p (t m j) -> p m t j", t=PACK, j=PACK)[:, m0:m1, t0:t1]
+            src = raw[:].rearrange("p j (m t) -> p m t j", t=PACK)[:, m0 - base : m1 - base, t0:t1]
+            if engine is nc.scalar:
+                nc.scalar.copy(dst, src)
+            else:
+                nc.vector.tensor_copy(dst, src)
+
+        cut = 96
+        lay(nc.vector, 0, w1_raw[0], 0, cut, 0, PACK)
+        lay(nc.scalar, 0, w1_raw[0], cut, P, 0, PACK)
+        quantize_x(1)
+        quantize(w1_codes[0][:], w1_scales[0][:], w1g[0][:])
+        for b in range(2):
+            m0, m1 = b * (P // 2), (b + 1) * (P // 2)
+            lay(nc.vector, 1, halves[b], m0, m1, 0, 2)
+            lay(nc.scalar, 1, halves[b], m0, m1, 2, PACK)
+            for t in range(PACK):
+                cols = slice(t * P + m0, t * P + m1)
+                quantize(w1_codes[1][:, cols], w1_scales[1][:, cols], w1g[1][:, (t * P + m0) * PACK : (t * P + m1) * PACK])
+
+        h = [keep.tile([P, S], F32, name=f"h{t}") for t in range(PACK)]
+        banks = []
+        for t in range(PACK):
+            w = S // 2 if t == 0 else S
+            banks.append([(c, w, psum.tile([P, w], F32, name=f"h_acc{t}_{c}")) for c in range(0, S, w)])
+        for s in range(PASSES):
+            for t in range(PACK):
+                for c, w, acc in banks[t]:
+                    nc.tensor.matmul_mx(
+                        out=acc[:],
+                        lhsT=w1_codes[s][:, t * P : (t + 1) * P].bitcast(FP8X4),
+                        lhsT_scale=w1_scales[s][:, t * P : (t + 1) * P],
+                        rhs=x_codes[s][:, c : c + w].bitcast(FP8X4),
+                        rhs_scale=x_scales[s][:, c : c + w],
+                        start=(s == 0),
+                        stop=(s == PASSES - 1),
+                    )
+        for t in range(PACK):
+            for c, w, acc in banks[t]:
+                if c == 0:
+                    nc.scalar.activation(h[t][:, c : c + w], acc[:], RELU)
+                else:
+                    nc.vector.tensor_scalar_max(h[t][:, c : c + w], acc[:], 0.0)
+
+        u = [keep.tile([P, PACK, V], F32, name=f"u{d}") for d in range(D)]
+        s01 = keep.tile([P, PACK, V], F32, name="s01")
+        w2g = keep.tile([P, N, PACK], BF16, name="w2g", align_bytes=64)
+        w2_codes = keep.tile([P, N], U32, name="w2_codes", align_bytes=64)
+        w2_scales = keep.tile([P, N], U8, name="w2_scales", align_bytes=64)
+        nc.scalar.copy(w2g[:], w2_raw[:].rearrange("p j m -> p m j"))
+        vh = V // 2
+
+        def fetch(t, d, v0, v1):
+            nc.vector.tensor_tensor(u[d][:, t, v0:v1], h[t][:].indirect(pos_t[d][:, v0 // 16 : v1 // 16]), gates[:, d, v0:v1], MULT)
+
+        def add_pair(t):
+            pair = slice(t, t + 2)
+            nc.vector.tensor_tensor(s01[:, pair, :], u[0][:, pair, :], u[1][:, pair, :], ADD)
+
+        for t in range(PACK - 1):
+            for d in range(D):
+                fetch(t, d, 0, V)
+            if t == 1:
+                add_pair(0)
+                quantize(w2_codes[:], w2_scales[:], w2g[:].rearrange("p m j -> p (m j)"))
+        fetch(PACK - 1, 0, 0, V)
+        fetch(PACK - 1, 1, 0, V)
+        fetch(PACK - 1, 2, 0, vh)
+        add_pair(2)
+        fetch(PACK - 1, 2, vh, V)
+
+        zg = keep.tile([P, V, PACK], BF16, name="zg", align_bytes=64)
+        z_codes = keep.tile([P, V], U32, name="z_codes", align_bytes=64)
+        z_scales = keep.tile([P, V], U8, name="z_scales", align_bytes=64)
+        for c in (0, vh):
+            nc.vector.tensor_tensor(
+                zg[:, c : c + vh, :],
+                s01[:, :, c : c + vh].rearrange("p t v -> p v t"),
+                u[2][:, :, c : c + vh].rearrange("p t v -> p v t"),
+                ADD,
+            )
+        for c in (0, vh):
+            quantize(z_codes[:, c : c + vh], z_scales[:, c : c + vh], zg[:, c : c + vh, :].rearrange("p v j -> p (v j)"))
+        for c in (0, vh):
+            acc = psum.tile([P, vh], F32, name=f"o_acc{c}")
+            nc.tensor.matmul_mx(
+                out=acc[:],
+                lhsT=w2_codes[:].bitcast(FP8X4),
+                lhsT_scale=w2_scales[:],
+                rhs=z_codes[:, c : c + vh].bitcast(FP8X4),
+                rhs_scale=z_scales[:, c : c + vh],
+                start=True,
+                stop=True,
+            )
+            res = keep.tile([P, vh], F32, name=f"res{c}")
+            if c == 0:
+                nc.scalar.copy(res[:], acc[:])
+            else:
+                nc.vector.tensor_copy(res[:], acc[:])
+            nc.sync.dma_start(out[:, c : c + vh], res[:])

@@ -37,12 +37,12 @@ def tile_picked_sage_relu_e_kernel(tc, xT, w1, w2, gate, offs, pos1, pos2, pos3,
         w2_raw = keep.tile([P, PACK, N], F32, name="w2_raw")
         gates = keep.tile([P, D, V], F32, name="gates")
 
+        nc.sync.dma_start(w1_raw[0][:], w1_rows[0])
         nc.sync.dma_start(xs[0][0][:], planes[0, 0])
         for d, p in enumerate((pos1, pos2, pos3)):
             nc.sync.dma_start(pos_t[d][:], p)
         for i in range(1, PASSES * PACK):
             nc.sync.dma_start(xs[i // PACK][i % PACK][:], planes[i // PACK, i % PACK])
-        nc.sync.dma_start(w1_raw[0][:], w1_rows[0])
         for u in range(2):
             nc.sync.dma_start(halves[u][:], w1_rows[1][:, :, u * (H // 2) : (u + 1) * (H // 2)])
         nc.sync.dma_start(gates[:], gate.rearrange("d p v -> p d v"))
@@ -61,30 +61,41 @@ def tile_picked_sage_relu_e_kernel(tc, xT, w1, w2, gate, offs, pos1, pos2, pos3,
         def quantize_x(s):
             quantize(x_codes[s][:], x_scales[s][:], xg[s][:].rearrange("p n j -> p (n j)"))
 
-        for i in range(PASSES * PACK):
-            s, j = i // PACK, i % PACK
-            nc.vector.tensor_copy(xg[s][:, :, j], xs[s][j][:].indirect(offs_t[:]))
-            if i == PACK:
-                quantize_x(0)
+        picked = [
+            keep.tile([P, PACK, S], F32, name="picked0", align_bytes=64),
+            keep.tile([P, 2, S], F32, name="picked1", align_bytes=64),
+        ]
 
-        def lay(engine, s, raw, m0, m1, t0, t1):
-            base = 0 if raw is w1_raw[0] else m0
-            dst = w1g[s][:].rearrange("p (t m j) -> p m t j", t=PACK, j=PACK)[:, m0:m1, t0:t1]
-            src = raw[:].rearrange("p j (m t) -> p m t j", t=PACK)[:, m0 - base : m1 - base, t0:t1]
-            if engine is nc.scalar:
-                nc.scalar.copy(dst, src)
-            else:
-                nc.vector.tensor_copy(dst, src)
+        def interleave(dst, src):
+            return dst.rearrange("p (c i) j -> p c j i", i=4), src.rearrange("p j (c i) -> p c j i", i=4)
 
-        cut = 96
-        lay(nc.vector, 0, w1_raw[0], 0, cut, 0, PACK)
-        lay(nc.scalar, 0, w1_raw[0], cut, P, 0, PACK)
+        def lay(s, raw, b0, m0, m1, t0, t1):
+            nc.scalar.copy(
+                w1g[s][:].rearrange("p (t m j) -> p m j t", t=PACK, j=PACK)[:, m0:m1, :, t0:t1],
+                raw[:].rearrange("p j (m t) -> p m j t", t=PACK)[:, m0 - b0 : m1 - b0, :, t0:t1],
+            )
+
+        lay(0, w1_raw[0], 0, 0, P, 0, PACK)
+        for j in range(PACK):
+            nc.vector.tensor_copy(picked[0][:, j, :], xs[0][j][:].indirect(offs_t[:]))
+            if j == 1:
+                quantize(w1_codes[0][:], w1_scales[0][:], w1g[0][:])
+        nc.scalar.copy(*interleave(xg[0][:], picked[0][:]))
+        nc.vector.tensor_copy(picked[1][:, 0, :], xs[1][0][:].indirect(offs_t[:]))
+        nc.vector.tensor_copy(picked[1][:, 1, :], xs[1][1][:].indirect(offs_t[:]))
+        nc.scalar.copy(*interleave(xg[1][:, :, 0:2], picked[1][:]))
+        quantize_x(0)
+        nc.vector.tensor_copy(xg[1][:, :, 2], xs[1][2][:].indirect(offs_t[:]))
+        nc.vector.tensor_copy(xg[1][:, :, 3], xs[1][3][:].indirect(offs_t[:]))
         quantize_x(1)
-        quantize(w1_codes[0][:], w1_scales[0][:], w1g[0][:])
+        half = P // 2
         for b in range(2):
-            m0, m1 = b * (P // 2), (b + 1) * (P // 2)
-            lay(nc.vector, 1, halves[b], m0, m1, 0, 2)
-            lay(nc.scalar, 1, halves[b], m0, m1, 2, PACK)
+            m0, m1 = b * half, (b + 1) * half
+            if b == 0:
+                lay(1, halves[b], m0, m0, m1, 0, PACK)
+            else:
+                lay(1, halves[b], m0, m0, m1, 0, 2)
+                lay(1, halves[b], m0, m0, m1, 2, PACK)
             for t in range(PACK):
                 cols = slice(t * P + m0, t * P + m1)
                 quantize(w1_codes[1][:, cols], w1_scales[1][:, cols], w1g[1][:, (t * P + m0) * PACK : (t * P + m1) * PACK])
@@ -118,7 +129,7 @@ def tile_picked_sage_relu_e_kernel(tc, xT, w1, w2, gate, offs, pos1, pos2, pos3,
         w2g = keep.tile([P, N, PACK], BF16, name="w2g", align_bytes=64)
         w2_codes = keep.tile([P, N], U32, name="w2_codes", align_bytes=64)
         w2_scales = keep.tile([P, N], U8, name="w2_scales", align_bytes=64)
-        nc.scalar.copy(w2g[:], w2_raw[:].rearrange("p j m -> p m j"))
+        nc.scalar.copy(*interleave(w2g[:], w2_raw[:]))
         vh = V // 2
 
         def fetch(t, d, v0, v1):
@@ -145,9 +156,8 @@ def tile_picked_sage_relu_e_kernel(tc, xT, w1, w2, gate, offs, pos1, pos2, pos3,
         z_scales = keep.tile([P, V], U8, name="z_scales", align_bytes=64)
         for c in (0, vh):
             nc.vector.tensor_tensor(
-                zg[:, c : c + vh, :],
-                s01[:, :, c : c + vh].rearrange("p t v -> p v t"),
-                u[2][:, :, c : c + vh].rearrange("p t v -> p v t"),
+                *interleave(zg[:, c : c + vh, :], s01[:, :, c : c + vh]),
+                u[2][:, :, c : c + vh].rearrange("p t (c i) -> p c t i", i=4),
                 ADD,
             )
         for c in (0, vh):

@@ -29,24 +29,31 @@ def tile_picked_sage_relu_e_kernel(tc, xT, w1, w2, gate, offs, pos1, pos2, pos3,
         pos_t = [keep.tile([P, V // 16], U16, name=f"pos_t{d}") for d in range(D)]
         nc.sync.dma_start(offs_t[:], offs)
 
-        planes = xT.rearrange("(s p j) t -> s j p t", p=P, j=PACK)
+        x_rows = xT.rearrange("(s p j) t -> s p j t", p=P, j=PACK)
         w1_rows = w1.rearrange("(s p j) c -> s p j c", p=P, j=PACK)
-        xs = [[keep.tile([P, T], F32, name=f"x{s}_{j}") for j in range(PACK)] for s in range(PASSES)]
-        w1_raw = [keep.tile([P, PACK, H], F32, name="w1_raw0")]
-        halves = [keep.tile([P, PACK, H // 2], F32, name=f"w1_raw1_{u}") for u in range(2)]
+        pieces = [[(0, 2), (2, 2)], [(0, 1), (1, 1), (2, 1), (3, 1)]]
+        w1_raw0 = keep.tile([P, PACK, H], F32, name="w1_raw0")
+        pairs = [keep.tile([P, 2, H], F32, name=f"w1_raw1_{b}") for b in range(2)]
         w2_raw = keep.tile([P, PACK, N], F32, name="w2_raw")
         gates = keep.tile([P, D, V], F32, name="gates")
+        plane = {}
 
-        nc.sync.dma_start(w1_raw[0][:], w1_rows[0])
-        nc.sync.dma_start(xs[0][0][:], planes[0, 0])
-        for d, p in enumerate((pos1, pos2, pos3)):
-            nc.sync.dma_start(pos_t[d][:], p)
-        for i in range(1, PASSES * PACK):
-            nc.sync.dma_start(xs[i // PACK][i % PACK][:], planes[i // PACK, i % PACK])
-        for u in range(2):
-            nc.sync.dma_start(halves[u][:], w1_rows[1][:, :, u * (H // 2) : (u + 1) * (H // 2)])
+        nc.sync.dma_start(w1_raw0[:], w1_rows[0])
+        for s in range(PASSES):
+            for j0, n in pieces[s]:
+                x_t = keep.tile([P, n, T], F32, name=f"x{s}_{j0}")
+                nc.sync.dma_start(x_t[:], x_rows[s][:, j0 : j0 + n, :])
+                for j in range(n):
+                    plane[s, j0 + j] = x_t[:, j, :]
+                if s == 0 and j0 == 0:
+                    for d, p in enumerate((pos1, pos2, pos3)):
+                        nc.sync.dma_start(pos_t[d][:], p)
+        for b in range(2):
+            nc.sync.dma_start(pairs[b][:], w1_rows[1][:, 2 * b : 2 * b + 2, :])
         nc.sync.dma_start(gates[:], gate.rearrange("d p v -> p d v"))
-        nc.sync.dma_start(w2_raw[:], w2.rearrange("(p j) m -> p j m", j=PACK))
+        w2_rows = w2.rearrange("(g t r) m -> t g r m", t=PACK, r=8)
+        for t in range(PACK):
+            nc.sync.dma_start(w2_raw[:, t, :], w2_rows[t])
 
         xg = [keep.tile([P, S, PACK], BF16, name=f"xg{s}", align_bytes=64) for s in range(PASSES)]
         x_codes = [keep.tile([P, S], U32, name=f"x_codes{s}", align_bytes=64) for s in range(PASSES)]
@@ -69,36 +76,31 @@ def tile_picked_sage_relu_e_kernel(tc, xT, w1, w2, gate, offs, pos1, pos2, pos3,
         def interleave(dst, src):
             return dst.rearrange("p (c i) j -> p c j i", i=4), src.rearrange("p j (c i) -> p c j i", i=4)
 
-        def lay(s, raw, b0, m0, m1, t0, t1):
-            nc.scalar.copy(
-                w1g[s][:].rearrange("p (t m j) -> p m j t", t=PACK, j=PACK)[:, m0:m1, :, t0:t1],
-                raw[:].rearrange("p j (m t) -> p m j t", t=PACK)[:, m0 - b0 : m1 - b0, :, t0:t1],
+        def lay(engine_copy, raw, s, j0, j1, t0, t1):
+            engine_copy(
+                w1g[s][:].rearrange("p (t g r j) -> p t g r j", t=PACK, r=8, j=PACK)[:, t0:t1, :, :, j0:j1],
+                raw.rearrange("p j (g t r) -> p t g r j", t=PACK, r=8)[:, t0:t1],
             )
 
-        lay(0, w1_raw[0], 0, 0, P, 0, PACK)
+        lay(nc.scalar.copy, w1_raw0[:], 0, 0, PACK, 0, PACK)
         for j in range(PACK):
-            nc.vector.tensor_copy(picked[0][:, j, :], xs[0][j][:].indirect(offs_t[:]))
+            nc.vector.tensor_copy(picked[0][:, j, :], plane[0, j].indirect(offs_t[:]))
             if j == 1:
                 quantize(w1_codes[0][:], w1_scales[0][:], w1g[0][:])
         nc.scalar.copy(*interleave(xg[0][:], picked[0][:]))
-        nc.vector.tensor_copy(picked[1][:, 0, :], xs[1][0][:].indirect(offs_t[:]))
-        nc.vector.tensor_copy(picked[1][:, 1, :], xs[1][1][:].indirect(offs_t[:]))
-        nc.scalar.copy(*interleave(xg[1][:, :, 0:2], picked[1][:]))
+        nc.vector.tensor_copy(picked[1][:, 0, :], plane[1, 0].indirect(offs_t[:]))
         quantize_x(0)
-        nc.vector.tensor_copy(xg[1][:, :, 2], xs[1][2][:].indirect(offs_t[:]))
-        nc.vector.tensor_copy(xg[1][:, :, 3], xs[1][3][:].indirect(offs_t[:]))
+        nc.vector.tensor_copy(picked[1][:, 1, :], plane[1, 1].indirect(offs_t[:]))
+        nc.scalar.copy(*interleave(xg[1][:, :, 0:2], picked[1][:]))
+        nc.vector.tensor_copy(xg[1][:, :, 2], plane[1, 2].indirect(offs_t[:]))
+        nc.vector.tensor_copy(xg[1][:, :, 3], plane[1, 3].indirect(offs_t[:]))
         quantize_x(1)
-        half = P // 2
-        for b in range(2):
-            m0, m1 = b * half, (b + 1) * half
-            if b == 0:
-                lay(1, halves[b], m0, m0, m1, 0, PACK)
-            else:
-                lay(1, halves[b], m0, m0, m1, 0, 2)
-                lay(1, halves[b], m0, m0, m1, 2, PACK)
-            for t in range(PACK):
-                cols = slice(t * P + m0, t * P + m1)
-                quantize(w1_codes[1][:, cols], w1_scales[1][:, cols], w1g[1][:, (t * P + m0) * PACK : (t * P + m1) * PACK])
+        lay(nc.scalar.copy, pairs[0][:], 1, 0, 2, 0, PACK)
+        for t in range(PACK):
+            lay(nc.scalar.copy if t else nc.vector.tensor_copy, pairs[1][:], 1, 2, 4, t, t + 1)
+        for t in range(PACK):
+            cols = slice(t * P, (t + 1) * P)
+            quantize(w1_codes[1][:, cols], w1_scales[1][:, cols], w1g[1][:, t * P * PACK : (t + 1) * P * PACK])
 
         h = [keep.tile([P, S], F32, name=f"h{t}") for t in range(PACK)]
         banks = []

@@ -45,12 +45,11 @@ def tile_picked_sage_relu_e_kernel(tc, xT, w1, w2, gate, offs, pos1, pos2, pos3,
                 nc.sync.dma_start(x_t[:], x_rows[s][:, j0 : j0 + n, :])
                 for j in range(n):
                     plane[s, j0 + j] = x_t[:, j, :]
-                if s == 0 and j0 == 0:
-                    for d, p in enumerate((pos1, pos2, pos3)):
-                        nc.sync.dma_start(pos_t[d][:], p)
         for b in range(2):
             nc.sync.dma_start(pairs[b][:], w1_rows[1][:, 2 * b : 2 * b + 2, :])
         nc.sync.dma_start(gates[:], gate.rearrange("d p v -> p d v"))
+        for d, p in enumerate((pos1, pos2, pos3)):
+            nc.sync.dma_start(pos_t[d][:], p)
         w2_rows = w2.rearrange("(g t r) m -> t g r m", t=PACK, r=8)
         for t in range(PACK):
             nc.sync.dma_start(w2_raw[:, t, :], w2_rows[t])
@@ -95,10 +94,15 @@ def tile_picked_sage_relu_e_kernel(tc, xT, w1, w2, gate, offs, pos1, pos2, pos3,
         nc.vector.tensor_copy(xg[1][:, :, 2], plane[1, 2].indirect(offs_t[:]))
         nc.vector.tensor_copy(xg[1][:, :, 3], plane[1, 3].indirect(offs_t[:]))
         quantize_x(1)
-        lay(nc.scalar.copy, pairs[0][:], 1, 0, 2, 0, PACK)
+        lay(nc.scalar.copy, pairs[0][:], 1, 0, 2, 0, 1)
+        lay(nc.scalar.copy, pairs[0][:], 1, 0, 2, 1, PACK)
         for t in range(PACK):
-            lay(nc.scalar.copy if t else nc.vector.tensor_copy, pairs[1][:], 1, 2, 4, t, t + 1)
-        for t in range(PACK):
+            lay(nc.scalar.copy if t >= 2 else nc.vector.tensor_copy, pairs[1][:], 1, 2, 4, t, t + 1)
+            if t != 1 and t != 2:
+                continue
+            cols = slice((t - 1) * P, t * P)
+            quantize(w1_codes[1][:, cols], w1_scales[1][:, cols], w1g[1][:, (t - 1) * P * PACK : t * P * PACK])
+        for t in (2, 3):
             cols = slice(t * P, (t + 1) * P)
             quantize(w1_codes[1][:, cols], w1_scales[1][:, cols], w1g[1][:, t * P * PACK : (t + 1) * P * PACK])
 

from contextlib import ExitStack

import concourse.mybir as mybir

K, T, D, S, V, H, N = 1024, 2048, 3, 512, 256, 512, 128
P = 128
PACK = 4
PASSES = K // (P * PACK)
FLOPS = 2 * K * S * H + 2 * H * V * N

F32 = mybir.dt.float32
BF16 = mybir.dt.bfloat16
U32 = mybir.dt.uint32
U16 = mybir.dt.uint16
U8 = mybir.dt.uint8
FP8X4 = mybir.dt.float8_e4m3fn_x4
ADD = mybir.AluOpType.add
MULT = mybir.AluOpType.mult
RELU = mybir.ActivationFunctionType.Relu


def tile_picked_sage_relu_e_kernel(tc, xT, w1, w2, gate, offs, pos1, pos2, pos3, out):
    nc = tc.nc
    with ExitStack() as ctx:
        keep = ctx.enter_context(tc.tile_pool(name="keep", bufs=1))
        psum = ctx.enter_context(tc.psum_pool(name="psum", bufs=1))

        offs_t = keep.tile([P, S // 16], U16, name="offs_t")
        pos_t = [keep.tile([P, V // 16], U16, name=f"pos_t{d}") for d in range(D)]
        nc.sync.dma_start(offs_t[:], offs)

        x_rows = xT.rearrange("(s p j) t -> s p j t", p=P, j=PACK)
        w1_rows = w1.rearrange("(s p j) c -> s p j c", p=P, j=PACK)
        pieces = [[(0, 2), (2, 2)], [(0, 1), (1, 1), (2, 1), (3, 1)]]
        w1_raw0 = keep.tile([P, PACK, H], F32, name="w1_raw0")
        pairs = [keep.tile([P, 2, H], F32, name=f"w1_raw1_{b}") for b in range(2)]
        w2_raw = keep.tile([P, PACK, N], F32, name="w2_raw")
        gates = keep.tile([P, D, V], F32, name="gates")
        plane = {}

        nc.sync.dma_start(w1_raw0[:], w1_rows[0])
        for s in range(PASSES):
            for j0, n in pieces[s]:
                x_t = keep.tile([P, n, T], F32, name=f"x{s}_{j0}")
                nc.sync.dma_start(x_t[:], x_rows[s][:, j0 : j0 + n, :])
                for j in range(n):
                    plane[s, j0 + j] = x_t[:, j, :]
        for b in range(2):
            nc.sync.dma_start(pairs[b][:], w1_rows[1][:, 2 * b : 2 * b + 2, :])
        nc.sync.dma_start(gates[:], gate.rearrange("d p v -> p d v"))
        for d, p in enumerate((pos1, pos2, pos3)):
            nc.sync.dma_start(pos_t[d][:], p)
        w2_rows = w2.rearrange("(g t r) m -> t g r m", t=PACK, r=8)
        for t in range(PACK):
            nc.sync.dma_start(w2_raw[:, t, :], w2_rows[t])

        xg = [keep.tile([P, S, PACK], BF16, name=f"xg{s}", align_bytes=64) for s in range(PASSES)]
        x_codes = [keep.tile([P, S], U32, name=f"x_codes{s}", align_bytes=64) for s in range(PASSES)]
        x_scales = [keep.tile([P, S], U8, name=f"x_scales{s}", align_bytes=64) for s in range(PASSES)]
        w1g = [keep.tile([P, H * PACK], BF16, name=f"w1g{s}", align_bytes=64) for s in range(PASSES)]
        w1_codes = [keep.tile([P, H], U32, name=f"w1_codes{s}", align_bytes=64) for s in range(PASSES)]
        w1_scales = [keep.tile([P, H], U8, name=f"w1_scales{s}", align_bytes=64) for s in range(PASSES)]

        def quantize(codes, scales, grouped):
            nc.vector.quantize_mx(out=codes.bitcast(FP8X4), scales=scales, in_=grouped)

        def quantize_x(s):
            quantize(x_codes[s][:], x_scales[s][:], xg[s][:].rearrange("p n j -> p (n j)"))

        picked = [
            keep.tile([P, PACK, S], F32, name="picked0", align_bytes=64),
            keep.tile([P, 2, S], F32, name="picked1", align_bytes=64),
        ]

        def interleave(dst, src):
            return dst.rearrange("p (c i) j -> p c j i", i=4), src.rearrange("p j (c i) -> p c j i", i=4)

        def lay(engine_copy, raw, s, j0, j1, t0, t1):
            engine_copy(
                w1g[s][:].rearrange("p (t g r j) -> p t g r j", t=PACK, r=8, j=PACK)[:, t0:t1, :, :, j0:j1],
                raw.rearrange("p j (g t r) -> p t g r j", t=PACK, r=8)[:, t0:t1],
            )

        lay(nc.scalar.copy, w1_raw0[:], 0, 0, PACK, 0, PACK)
        for j in range(PACK):
            nc.vector.tensor_copy(picked[0][:, j, :], plane[0, j].indirect(offs_t[:]))
            if j == 1:
                quantize(w1_codes[0][:], w1_scales[0][:], w1g[0][:])
        nc.scalar.copy(*interleave(xg[0][:], picked[0][:]))
        nc.vector.tensor_copy(picked[1][:, 0, :], plane[1, 0].indirect(offs_t[:]))
        quantize_x(0)
        nc.vector.tensor_copy(picked[1][:, 1, :], plane[1, 1].indirect(offs_t[:]))
        nc.scalar.copy(*interleave(xg[1][:, :, 0:2], picked[1][:]))
        nc.vector.tensor_copy(xg[1][:, :, 2], plane[1, 2].indirect(offs_t[:]))
        nc.vector.tensor_copy(xg[1][:, :, 3], plane[1, 3].indirect(offs_t[:]))
        quantize_x(1)
        lay(nc.scalar.copy, pairs[0][:], 1, 0, 2, 0, 1)
        lay(nc.scalar.copy, pairs[0][:], 1, 0, 2, 1, PACK)
        for t in range(PACK):
            lay(nc.scalar.copy if t >= 2 else nc.vector.tensor_copy, pairs[1][:], 1, 2, 4, t, t + 1)
            if t != 1 and t != 2:
                continue
            cols = slice((t - 1) * P, t * P)
            quantize(w1_codes[1][:, cols], w1_scales[1][:, cols], w1g[1][:, (t - 1) * P * PACK : t * P * PACK])
        for t in (2, 3):
            cols = slice(t * P, (t + 1) * P)
            quantize(w1_codes[1][:, cols], w1_scales[1][:, cols], w1g[1][:, t * P * PACK : (t + 1) * P * PACK])

        h = [keep.tile([P, S], F32, name=f"h{t}") for t in range(PACK)]
        banks = []
        for t in range(PACK):
            w = S // 2 if t == 0 else S
            banks.append([(c, w, psum.tile([P, w], F32, name=f"h_acc{t}_{c}")) for c in range(0, S, w)])
        for s in range(PASSES):
            for t in range(PACK):
                for c, w, acc in banks[t]:
                    nc.tensor.matmul_mx(
                        out=acc[:],
                        lhsT=w1_codes[s][:, t * P : (t + 1) * P].bitcast(FP8X4),
                        lhsT_scale=w1_scales[s][:, t * P : (t + 1) * P],
                        rhs=x_codes[s][:, c : c + w].bitcast(FP8X4),
                        rhs_scale=x_scales[s][:, c : c + w],
                        start=(s == 0),
                        stop=(s == PASSES - 1),
                    )
        for t in range(PACK):
            for c, w, acc in banks[t]:
                if c == 0:
                    nc.scalar.activation(h[t][:, c : c + w], acc[:], RELU)
                else:
                    nc.vector.tensor_scalar_max(h[t][:, c : c + w], acc[:], 0.0)

        u = [keep.tile([P, PACK, V], F32, name=f"u{d}") for d in range(D)]
        s01 = keep.tile([P, PACK, V], F32, name="s01")
        w2g = keep.tile([P, N, PACK], BF16, name="w2g", align_bytes=64)
        w2_codes = keep.tile([P, N], U32, name="w2_codes", align_bytes=64)
        w2_scales = keep.tile([P, N], U8, name="w2_scales", align_bytes=64)
        nc.scalar.copy(*interleave(w2g[:], w2_raw[:]))
        vh = V // 2

        def fetch(t, d, v0, v1):
            nc.vector.tensor_tensor(u[d][:, t, v0:v1], h[t][:].indirect(pos_t[d][:, v0 // 16 : v1 // 16]), gates[:, d, v0:v1], MULT)

        def add_pair(t):
            pair = slice(t, t + 2)
            nc.vector.tensor_tensor(s01[:, pair, :], u[0][:, pair, :], u[1][:, pair, :], ADD)

        for t in range(PACK - 1):
            for d in range(D):
                fetch(t, d, 0, V)
            if t == 1:
                add_pair(0)
                quantize(w2_codes[:], w2_scales[:], w2g[:].rearrange("p m j -> p (m j)"))
        fetch(PACK - 1, 0, 0, V)
        fetch(PACK - 1, 1, 0, V)
        fetch(PACK - 1, 2, 0, vh)
        add_pair(2)
        fetch(PACK - 1, 2, vh, V)

        zg = keep.tile([P, V, PACK], BF16, name="zg", align_bytes=64)
        z_codes = keep.tile([P, V], U32, name="z_codes", align_bytes=64)
        z_scales = keep.tile([P, V], U8, name="z_scales", align_bytes=64)
        for c in (0, vh):
            nc.vector.tensor_tensor(
                *interleave(zg[:, c : c + vh, :], s01[:, :, c : c + vh]),
                u[2][:, :, c : c + vh].rearrange("p t (c i) -> p c t i", i=4),
                ADD,
            )
        for c in (0, vh):
            quantize(z_codes[:, c : c + vh], z_scales[:, c : c + vh], zg[:, c : c + vh, :].rearrange("p v j -> p (v j)"))
        for c in (0, vh):
            acc = psum.tile([P, vh], F32, name=f"o_acc{c}")
            nc.tensor.matmul_mx(
                out=acc[:],
                lhsT=w2_codes[:].bitcast(FP8X4),
                lhsT_scale=w2_scales[:],
                rhs=z_codes[:, c : c + vh].bitcast(FP8X4),
                rhs_scale=z_scales[:, c : c + vh],
                start=True,
                stop=True,
            )
            res = keep.tile([P, vh], F32, name=f"res{c}")
            if c == 0:
                nc.scalar.copy(res[:], acc[:])
            else:
                nc.vector.tensor_copy(res[:], acc[:])
            nc.sync.dma_start(out[:, c : c + vh], res[:])
